import numpy as np
import ml_dtypes

BF16 = ml_dtypes.bfloat16


def bf(x):
    return np.asarray(x, np.float32).astype(BF16)


def f32(x):
    return np.asarray(x, np.float32)


def f64(x):
    return np.asarray(x).astype(np.float64)


def striped(idx):
    return np.concatenate([l.reshape(-1, 16).T for l in idx])


def rows(idx, k):
    return np.tile(np.repeat(idx, 16, axis=0), (k // (16 * 8), 1))


def look(tab, idx):
    return np.take_along_axis(f64(tab), rows(idx, len(tab)), axis=1)


K, S, D, V, N, M = 128, 2048, 2, 512, 1024, 512


def setup_inputs():
    return {"tab": f32(np.random.standard_normal((K, S))), "x0": f32(np.random.standard_normal((K, V))), "w": bf(np.random.standard_normal((K, M)) / np.sqrt(K)), "offs": striped(np.stack([np.random.permutation(S)[:N] for _ in range(8)]))}


def reference(tab, x0, w, offs):
    idx = np.stack([g.T.reshape(-1) for g in np.split(offs, 8)])
    x = f64(x0)
    for d in range(D):
        x = np.maximum(x, look(tab, idx[:, d * V:(d + 1) * V]))
    y = f64(w).T @ x
    return y

@@ -1,0 +1,51 @@
+import concourse.mybir as mybir
+
+F32, BF16, U16 = mybir.dt.float32, mybir.dt.bfloat16, mybir.dt.uint16
+LARGEST = mybir.AluOpType.max
+
+P = 128
+S = 2048
+V = 512
+D = 2
+M = 512
+
+FLOPS = 2 * P * M * V
+
+
+def tile_lookup_pool_max_none_kernel(tc, tab, x0, w, offs, out):
+    nc = tc.nc
+    list_columns = V // 16
+    with (
+        tc.tile_pool(name="held", bufs=1) as held,
+        tc.tile_pool(name="ring", bufs=4) as ring,
+        tc.psum_pool(name="psum", bufs=4) as psum,
+    ):
+        offsets = held.tile([P, D * list_columns], U16, name="offsets")
+        nc.sync.dma_start(offsets[:], offs)
+        table = held.tile([P, S], F32, name="table")
+        nc.sync.dma_start(table[:], tab)
+        centre = held.tile([P, V], F32, name="centre")
+        nc.sync.dma_start(centre[:], x0)
+        weights = held.tile([P, M], BF16, name="weights")
+        nc.sync.dma_start(weights[:], w)
+
+        largest = centre
+        for d in range(D):
+            pooled = held.tile([P, V], F32, name=f"pooled{d}")
+            picked = table[:].indirect(offsets[:, d * list_columns : (d + 1) * list_columns])
+            nc.vector.tensor_tensor(pooled[:], picked, largest[:], LARGEST)
+            largest = pooled
+
+        x = held.tile([P, V], BF16, name="x")
+        nc.vector.tensor_copy(x[:], largest[:])
+
+        for b in range(M // P):
+            rows = slice(b * P, (b + 1) * P)
+            product = psum.tile([P, V], F32, name="product")
+            nc.tensor.matmul(product[:], weights[:, rows], x[:])
+            result = ring.tile([P, V], F32, name="result")
+            if b % 2 == 0:
+                nc.scalar.copy(result[:], product[:])
+            else:
+                nc.vector.tensor_copy(result[:], product[:])
+            nc.sync.dma_start(out[rows, :], result[:])

@@ -15,6 +15,7 @@ FLOPS = 2 * P * M * V
 def tile_lookup_pool_max_none_kernel(tc, tab, x0, w, offs, out):
     nc = tc.nc
     list_columns = V // 16
+    half = V // 2
     with (
         tc.tile_pool(name="held", bufs=1) as held,
         tc.tile_pool(name="ring", bufs=4) as ring,
@@ -36,16 +37,18 @@ def tile_lookup_pool_max_none_kernel(tc, tab, x0, w, offs, out):
             nc.vector.tensor_tensor(pooled[:], picked, largest[:], LARGEST)
             largest = pooled
 
-        x = held.tile([P, V], BF16, name="x")
-        nc.vector.tensor_copy(x[:], largest[:])
+        left = held.tile([P, half], BF16, name="left")
+        nc.vector.tensor_copy(left[:], largest[:, :half])
+        right = held.tile([P, half], BF16, name="right")
+        nc.vector.tensor_copy(right[:], largest[:, half:])
 
         for b in range(M // P):
             rows = slice(b * P, (b + 1) * P)
-            product = psum.tile([P, V], F32, name="product")
-            nc.tensor.matmul(product[:], weights[:, rows], x[:])
             result = ring.tile([P, V], F32, name="result")
-            if b % 2 == 0:
-                nc.scalar.copy(result[:], product[:])
-            else:
-                nc.vector.tensor_copy(result[:], product[:])
+            product_left = psum.tile([P, half], F32, name="product_left")
+            nc.tensor.matmul(product_left[:], weights[:, rows], left[:])
+            nc.scalar.copy(result[:, :half], product_left[:])
+            product_right = psum.tile([P, half], F32, name="product_right")
+            nc.tensor.matmul(product_right[:], weights[:, rows], right[:])
+            nc.vector.tensor_copy(result[:, half:], product_right[:])
             nc.sync.dma_start(out[rows, :], result[:])

@@ -19,7 +19,8 @@ def tile_lookup_pool_max_none_kernel(tc, tab, x0, w, offs, out):
     with (
         tc.tile_pool(name="held", bufs=1) as held,
         tc.tile_pool(name="ring", bufs=4) as ring,
-        tc.psum_pool(name="psum", bufs=4) as psum,
+        tc.psum_pool(name="psum", bufs=3) as psum,
+        tc.psum_pool(name="idle", bufs=1) as idle,
     ):
         offsets = held.tile([P, D * list_columns], U16, name="offsets")
         nc.sync.dma_start(offsets[:], offs)
@@ -29,6 +30,10 @@ def tile_lookup_pool_max_none_kernel(tc, tab, x0, w, offs, out):
         nc.sync.dma_start(centre[:], x0)
         weights = held.tile([P, M], BF16, name="weights")
         nc.sync.dma_start(weights[:], w)
+
+        unread = idle.tile([P, M], F32, name="unread")
+        for repeat in range(6):
+            nc.tensor.matmul(unread[:], weights[:, :P], weights[:])
 
         largest = centre
         for d in range(D):

import concourse.mybir as mybir

F32, BF16, U16 = mybir.dt.float32, mybir.dt.bfloat16, mybir.dt.uint16
LARGEST = mybir.AluOpType.max

P = 128
S = 2048
V = 512
D = 2
M = 512

FLOPS = 2 * P * M * V


def tile_lookup_pool_max_none_kernel(tc, tab, x0, w, offs, out):
    nc = tc.nc
    list_columns = V // 16
    half = V // 2
    with (
        tc.tile_pool(name="held", bufs=1) as held,
        tc.tile_pool(name="ring", bufs=4) as ring,
        tc.psum_pool(name="psum", bufs=3) as psum,
        tc.psum_pool(name="idle", bufs=1) as idle,
    ):
        offsets = held.tile([P, D * list_columns], U16, name="offsets")
        nc.sync.dma_start(offsets[:], offs)
        table = held.tile([P, S], F32, name="table")
        nc.sync.dma_start(table[:], tab)
        centre = held.tile([P, V], F32, name="centre")
        nc.sync.dma_start(centre[:], x0)
        weights = held.tile([P, M], BF16, name="weights")
        nc.sync.dma_start(weights[:], w)

        unread = idle.tile([P, M], F32, name="unread")
        for repeat in range(6):
            nc.tensor.matmul(unread[:], weights[:, :P], weights[:])

        largest = centre
        for d in range(D):
            pooled = held.tile([P, V], F32, name=f"pooled{d}")
            picked = table[:].indirect(offsets[:, d * list_columns : (d + 1) * list_columns])
            nc.vector.tensor_tensor(pooled[:], picked, largest[:], LARGEST)
            largest = pooled

        left = held.tile([P, half], BF16, name="left")
        nc.vector.tensor_copy(left[:], largest[:, :half])
        right = held.tile([P, half], BF16, name="right")
        nc.vector.tensor_copy(right[:], largest[:, half:])

        for b in range(M // P):
            rows = slice(b * P, (b + 1) * P)
            result = ring.tile([P, V], F32, name="result")
            product_left = psum.tile([P, half], F32, name="product_left")
            nc.tensor.matmul(product_left[:], weights[:, rows], left[:])
            nc.scalar.copy(result[:, :half], product_left[:])
            product_right = psum.tile([P, half], F32, name="product_right")
            nc.tensor.matmul(product_right[:], weights[:, rows], right[:])
            nc.vector.tensor_copy(result[:, half:], product_right[:])
            nc.sync.dma_start(out[rows, :], result[:])
